import numpy as np
import ml_dtypes


def mxq(x, axis, fmt="e4m3"):
    dtype, down = {"e4m3": (ml_dtypes.float8_e4m3fn, 7), "e5m2": (ml_dtypes.float8_e5m2, 14)}[fmt]
    v = np.moveaxis(np.asarray(x, np.float32).astype(ml_dtypes.bfloat16).astype(np.float64), axis, -1)
    blocks = v.reshape(v.shape[:-1] + (-1, 32))
    amax = np.abs(blocks).max(-1, keepdims=True)
    byte = np.maximum(np.where(amax > 0, np.frexp(amax)[1] - 1 + 127, 0) - down, 1)
    scale = np.exp2(byte - 127.0)
    codes = (blocks / scale).astype(np.float32).astype(dtype).astype(np.float64)
    return np.moveaxis((codes * scale).reshape(v.shape), -1, axis)


WIDE = False


def mx_kscale(k):
    if not WIDE:
        return np.ones(k)
    levels = np.array([10, -10, 5, -5, 0])
    if k % 512:
        return np.exp2(np.random.permutation(np.resize(levels, k // 32))).repeat(32)
    a = np.empty((k // 512, 16))
    for p in range(k // 512):
        a[p, :8] = np.random.permutation(np.resize(levels, 8))
        for g in range(8):
            far = levels[np.abs(levels - a[p, g]) >= 10]
            a[p, g + 8] = far[np.random.randint(len(far))]
    return np.exp2(a.ravel()).repeat(32)


def f64(x):
    return np.asarray(x).astype(np.float64)


def striped(idx):
    return np.tile(np.asarray(idx).reshape(-1, 16).T, (8, 1)).astype(np.uint16)


def unstriped(offs):
    return offs[:16].T.reshape(-1).astype(np.int64)


B, N, T, D, DV, NQ = 1, 512, 2048, 1024, 128, 128


def setup_inputs():
    n = np.random.standard_normal
    idx = np.sort(np.random.permutation(T)[:B * N].reshape(B, N), axis=1).reshape(-1)
    s = mx_kscale(D)[:, None]
    u = np.ones(T)
    u[idx] = mx_kscale(B * N)
    r = np.random.uniform(0.5, 2.0, T)
    k = n((D, T)) / s
    v = n((DV, T)) / (u * r)
    when = np.zeros(T)
    when[idx] = np.sort(np.random.permutation(2 * N)[:B * N])
    return {
        "qT": (n((B, D, NQ)) * s * (1.00 / np.sqrt(D))).astype(np.float32),
        "kT": k.astype(np.float32),
        "vT": v.astype(np.float32),
        "vs": np.tile(u * r, (128, 1)).astype(np.float32),
        "pos": np.tile(when, (128, 1)).astype(np.float32),
        "slope": np.exp2(-np.random.randint(8, 13, (B, NQ, 1))).astype(np.float32),
        "offs": striped(idx),
    }


def reference(qT, kT, vT, vs, pos, slope, offs):
    idx = unstriped(offs)
    k = f64(kT)
    v = f64(vT)
    pick = lambda x: x[:, idx].reshape(x.shape[0], B, N).transpose(1, 0, 2)
    q = f64(qT)
    score = mxq(q, 1, "e4m3").transpose(0, 2, 1) @ mxq(pick(k), 1, "e4m3")
    score = score + f64(slope) * pick(f64(pos))[:, :1, :]
    m = score.max(-1, keepdims=True)
    p = np.exp(score - m)
    total = p.sum(-1, keepdims=True)
    w = p * pick(f64(vs))[:, :1, :]
    y = mxq(w, 2, "e4m3") @ mxq(pick(v).transpose(0, 2, 1), 1, "e4m3")
    y = y / total
    return y

@@ -1,0 +1,216 @@
+from contextlib import ExitStack
+
+import concourse.mybir as mybir
+from concourse.masks import make_identity
+
+P = 128
+PACK = 4
+D, T, N, NQ, DV = 1024, 2048, 512, 128, 128
+PASSES = D // (P * PACK)
+HALF = N // 2
+SUB = N // PACK
+
+F32 = mybir.dt.float32
+BF16 = mybir.dt.bfloat16
+U32 = mybir.dt.uint32
+U16 = mybir.dt.uint16
+U8 = mybir.dt.uint8
+FP8X4 = mybir.dt.float8_e4m3fn_x4
+ALU = mybir.AluOpType
+ACT = mybir.ActivationFunctionType
+AXIS = mybir.AxisListType
+
+FLOPS = 2 * NQ * N * (D + DV)
+BYTES = 4 * (D * NQ + D * T + DV * T + 2 * T + NQ + NQ * DV) + 2 * P * (N // 16)
+
+
+def tile_attend_alibi_srt_kernel(tc, qT, kT, vT, vs, pos, slope, offs, out):
+    nc = tc.nc
+    with ExitStack() as ctx:
+        held = ctx.enter_context(tc.tile_pool(name="held", bufs=1))
+        psum = ctx.enter_context(tc.psum_pool(name="psum", bufs=1))
+
+        offsets = held.tile([P, N // 16], U16, name="offsets")
+        nc.sync.dma_start(offsets[:], offs)
+
+        dummy = held.tile([P, 1], F32, name="dummy")
+        nc.vector.memset(dummy[:], 0.0)
+        nc.scalar.activation(out=dummy[:], in_=dummy[:], func=ACT.Exp)
+
+        pos_pool = held.tile([P, T], F32, name="pos_pool")
+        vs_pool = held.tile([P, T], F32, name="vs_pool")
+        slope_col = held.tile([P, 1], F32, name="slope_col")
+        nc.scalar.dma_start(slope_col[:], slope[0])
+        nc.vector.memset(pos_pool[:], 0.0)
+        nc.gpsimd.memset(vs_pool[:], 0.0)
+
+        planes = kT.rearrange("(g p j) t -> g j p t", g=PASSES, j=PACK)
+        k_pool = []
+        q_raw = held.tile([P, PASSES, PACK, NQ], F32, name="q_raw")
+        for g in range(PASSES):
+            for j in range(PACK):
+                plane = held.tile([P, T], F32, name=f"plane{g}{j}")
+                nc.sync.dma_start(plane[:], planes[g, j])
+                k_pool.append(plane)
+                if g == 0 and j == 0:
+                    nc.sync.dma_start(pos_pool[0:1, :], pos[0:1, :])
+                    nc.sync.dma_start(vs_pool[0:1, :], vs[0:1, :])
+                    nc.sync.dma_start(q_raw[:], qT[0].rearrange("(g p j) q -> p g j q", g=PASSES, j=PACK))
+        v_pool = held.tile([P, T], F32, name="v_pool")
+        nc.sync.dma_start(v_pool[:], vT)
+
+        ident = held.tile([P, P], F32, name="ident")
+        make_identity(nc, ident[:])
+        ident_bf = held.tile([P, P], BF16, name="ident_bf")
+        make_identity(nc, ident_bf[:])
+
+        score = [psum.tile([NQ, HALF], F32, name=f"score{h}") for h in range(2)]
+        k_bf = [held.tile([P, N, PACK], BF16, name=f"k_bf{g}", align_bytes=64) for g in range(PASSES)]
+        k_codes = [held.tile([P, N], U32, name=f"k_codes{g}", align_bytes=64) for g in range(PASSES)]
+        k_scales = [held.tile([P, N], U8, name=f"k_scales{g}", align_bytes=64) for g in range(PASSES)]
+
+        def score_pass(g, h):
+            cols = slice(h * HALF, (h + 1) * HALF)
+            rows = slice(g * NQ, (g + 1) * NQ)
+            nc.tensor.matmul_mx(
+                out=score[h][:],
+                lhsT=q_codes[:, rows].bitcast(FP8X4),
+                lhsT_scale=q_scales[:, rows],
+                rhs=k_codes[g][:, cols].bitcast(FP8X4),
+                rhs_scale=k_scales[g][:, cols],
+                start=(g == 0),
+                stop=(g == PASSES - 1),
+            )
+
+        g4 = held.tile([P, PACK, N], F32, name="g4")
+        nc.vector.tensor_copy(out=g4[:, 0, :], in_=k_pool[0][:].indirect(offsets[:]))
+
+        pos_g = held.tile([P, N], F32, name="pos_g")
+        nc.vector.tensor_copy(out=pos_g[:], in_=pos_pool[:].indirect(offsets[:]))
+        vs_g = held.tile([P, N], F32, name="vs_g")
+        nc.vector.tensor_copy(out=vs_g[:], in_=vs_pool[:].indirect(offsets[:]))
+
+        pos_tp = psum.tile([P, PACK, P], F32, name="pos_tp")
+        pos_v = pos_g[:].rearrange("p (s t) -> p t s", t=PACK)
+        for t in range(PACK):
+            nc.tensor.transpose(pos_tp[:, t, :], pos_v[:, t, :], ident[:])
+        pos_col = held.tile([P, PACK], F32, name="pos_col")
+        nc.scalar.copy(pos_col[:], pos_tp[:, :, 0])
+        vs_tp = psum.tile([P, PACK, P], F32, name="vs_tp")
+        vs_v = vs_g[:].rearrange("p (s t) -> p t s", t=PACK)
+        for t in range(PACK):
+            nc.tensor.transpose(vs_tp[:, t, :], vs_v[:, t, :], ident[:])
+        vs_col = held.tile([P, PACK], F32, name="vs_col")
+        nc.scalar.copy(vs_col[:], vs_tp[:, :, 0])
+
+        pos_row = psum.tile([P, PACK, SUB], F32, name="pos_row")
+        for t in range(PACK):
+            nc.tensor.transpose(pos_row[:, t, :], pos_col[:, t : t + 1].to_broadcast([P, P]), ident[:])
+        neg_bias = held.tile([P, PACK, SUB], F32, name="neg_bias")
+        nc.vector.tensor_scalar(neg_bias[:], pos_row[:], slope_col[:, 0:1], -1.0, ALU.mult, ALU.mult)
+
+        q_bf = held.tile([P, PASSES, NQ, PACK], BF16, name="q_bf", align_bytes=64)
+        for g in range(PASSES):
+            nc.scalar.copy(q_bf[:, g, :, :], q_raw[:, g, :, :].rearrange("p j q -> p q j"))
+        q_codes = held.tile([P, PASSES * NQ], U32, name="q_codes", align_bytes=64)
+        q_scales = held.tile([P, PASSES * NQ], U8, name="q_scales", align_bytes=64)
+        nc.vector.quantize_mx(
+            out=q_codes[:].bitcast(FP8X4), scales=q_scales[:], in_=q_bf[:].rearrange("p g q j -> p (g q j)")
+        )
+
+        for j in range(1, PACK):
+            nc.vector.tensor_copy(out=g4[:, j, :], in_=k_pool[j][:].indirect(offsets[:]))
+        nc.scalar.copy(k_bf[0][:], g4[:].rearrange("p j s -> p s j"))
+        nc.vector.quantize_mx(
+            out=k_codes[0][:].bitcast(FP8X4), scales=k_scales[0][:], in_=k_bf[0][:].rearrange("p s j -> p (s j)")
+        )
+        for h in range(2):
+            score_pass(0, h)
+
+        g2 = held.tile([P, 2, N], F32, name="g2")
+        for j in range(2):
+            nc.vector.tensor_copy(out=g2[:, j, :], in_=k_pool[PACK + j][:].indirect(offsets[:]))
+        nc.scalar.copy(k_bf[1][:, :, 0:2], g2[:].rearrange("p j s -> p s j"))
+        nc.vector.tensor_copy(out=k_bf[1][:, :, 2], in_=k_pool[PACK + 2][:].indirect(offsets[:]))
+        for h in range(2):
+            cols = slice(h * HALF, (h + 1) * HALF)
+            list_part = offsets[:, h * (HALF // 16) : (h + 1) * (HALF // 16)]
+            nc.vector.tensor_copy(out=k_bf[1][:, cols, 3], in_=k_pool[PACK + 3][:].indirect(list_part))
+        for h in range(2):
+            cols = slice(h * HALF, (h + 1) * HALF)
+            nc.vector.quantize_mx(
+                out=k_codes[1][:, cols].bitcast(FP8X4),
+                scales=k_scales[1][:, cols],
+                in_=k_bf[1][:, cols, :].rearrange("p s j -> p (s j)"),
+            )
+            score_pass(1, h)
+
+        neg_s = held.tile([NQ, PACK, SUB], F32, name="neg_s")
+        for h in range(2):
+            part = slice(h * (SUB // 2), (h + 1) * (SUB // 2))
+            nc.vector.tensor_tensor(
+                neg_s[:, :, part],
+                neg_bias[:, :, part],
+                score[h][:].rearrange("q (s t) -> q t s", t=PACK),
+                ALU.subtract,
+            )
+        neg_m = held.tile([NQ, 1], F32, name="neg_m")
+        nc.vector.tensor_reduce(neg_m[:], neg_s[:].rearrange("q t s -> q (t s)"), AXIS.X, ALU.min)
+        p = held.tile([NQ, PACK, SUB], F32, name="p")
+        l_part = held.tile([NQ, 2], F32, name="l_part")
+        w_tp = psum.tile([P, PACK, NQ], F32, name="w_tp")
+        for h in range(2):
+            nc.scalar.activation(
+                out=p[:, 2 * h : 2 * h + 2, :],
+                in_=neg_s[:, 2 * h : 2 * h + 2, :],
+                func=ACT.Exp,
+                bias=neg_m[:, 0:1],
+                scale=-1.0,
+                accum_out=l_part[:, h : h + 1],
+            )
+            for t in (2 * h, 2 * h + 1):
+                nc.tensor.transpose(w_tp[:, t, :], p[:, t, :], ident[:])
+
+        v_bf = held.tile([DV, PACK, SUB], BF16, name="v_bf")
+        nc.vector.tensor_copy(out=v_bf[:].rearrange("e t s -> e s t"), in_=v_pool[:].indirect(offsets[:]))
+        v_tp = psum.tile([P, PACK, DV], BF16, name="v_tp")
+        for t in range(PACK):
+            nc.tensor.transpose(v_tp[:, t, :], v_bf[:, t, :], ident_bf[:])
+        v_rows = held.tile([P, DV, PACK], BF16, name="v_rows", align_bytes=64)
+        nc.scalar.copy(v_rows[:], v_tp[:].rearrange("s t e -> s e t"))
+
+        w_bf = held.tile([P, NQ, PACK], BF16, name="w_bf", align_bytes=64)
+        nc.vector.tensor_tensor(
+            w_bf[:],
+            w_tp[:].rearrange("s t q -> s q t"),
+            vs_col[:].unsqueeze(1).to_broadcast([P, NQ, PACK]),
+            ALU.mult,
+        )
+        v_codes = held.tile([P, DV], U32, name="v_codes", align_bytes=64)
+        v_scales = held.tile([P, DV], U8, name="v_scales", align_bytes=64)
+        nc.vector.quantize_mx(
+            out=v_codes[:].bitcast(FP8X4), scales=v_scales[:], in_=v_rows[:].rearrange("s e t -> s (e t)")
+        )
+        w_codes = held.tile([P, NQ], U32, name="w_codes", align_bytes=64)
+        w_scales = held.tile([P, NQ], U8, name="w_scales", align_bytes=64)
+        nc.vector.quantize_mx(
+            out=w_codes[:].bitcast(FP8X4), scales=w_scales[:], in_=w_bf[:].rearrange("s q t -> s (q t)")
+        )
+        total = held.tile([NQ, 1], F32, name="total")
+        nc.vector.tensor_tensor(total[:], l_part[:, 0:1], l_part[:, 1:2], ALU.add)
+        inverse = held.tile([NQ, 1], F32, name="inverse")
+        nc.vector.reciprocal(inverse[:], total[:])
+
+        y = psum.tile([NQ, DV], F32, name="y")
+        nc.tensor.matmul_mx(
+            out=y[:],
+            lhsT=w_codes[:].bitcast(FP8X4),
+            lhsT_scale=w_scales[:],
+            rhs=v_codes[:].bitcast(FP8X4),
+            rhs_scale=v_scales[:],
+            start=True,
+            stop=True,
+        )
+        result = held.tile([NQ, DV], F32, name="result")
+        nc.vector.tensor_scalar(result[:], y[:], inverse[:, 0:1], None, ALU.mult)
+        nc.sync.dma_start(out[0], result[:])

@@ -46,7 +46,8 @@ def tile_attend_alibi_srt_kernel(tc, qT, kT, vT, vs, pos, slope, offs, out):
 
         planes = kT.rearrange("(g p j) t -> g j p t", g=PASSES, j=PACK)
         k_pool = []
-        q_raw = held.tile([P, PASSES, PACK, NQ], F32, name="q_raw")
+        q_rows = qT[0].rearrange("(g p j) q -> g p j q", g=PASSES, j=PACK)
+        q_raw = [held.tile([P, PACK, NQ], F32, name=f"q_raw{g}") for g in range(PASSES)]
         for g in range(PASSES):
             for j in range(PACK):
                 plane = held.tile([P, T], F32, name=f"plane{g}{j}")
@@ -55,7 +56,8 @@ def tile_attend_alibi_srt_kernel(tc, qT, kT, vT, vs, pos, slope, offs, out):
                 if g == 0 and j == 0:
                     nc.sync.dma_start(pos_pool[0:1, :], pos[0:1, :])
                     nc.sync.dma_start(vs_pool[0:1, :], vs[0:1, :])
-                    nc.sync.dma_start(q_raw[:], qT[0].rearrange("(g p j) q -> p g j q", g=PASSES, j=PACK))
+                    nc.sync.dma_start(q_raw[0][:], q_rows[0])
+        nc.sync.dma_start(q_raw[1][:], q_rows[1])
         v_pool = held.tile([P, T], F32, name="v_pool")
         nc.sync.dma_start(v_pool[:], vT)
 
@@ -71,11 +73,10 @@ def tile_attend_alibi_srt_kernel(tc, qT, kT, vT, vs, pos, slope, offs, out):
 
         def score_pass(g, h):
             cols = slice(h * HALF, (h + 1) * HALF)
-            rows = slice(g * NQ, (g + 1) * NQ)
             nc.tensor.matmul_mx(
                 out=score[h][:],
-                lhsT=q_codes[:, rows].bitcast(FP8X4),
-                lhsT_scale=q_scales[:, rows],
+                lhsT=q_codes[g][:].bitcast(FP8X4),
+                lhsT_scale=q_scales[g][:],
                 rhs=k_codes[g][:, cols].bitcast(FP8X4),
                 rhs_scale=k_scales[g][:, cols],
                 start=(g == 0),
@@ -90,7 +91,7 @@ def tile_attend_alibi_srt_kernel(tc, qT, kT, vT, vs, pos, slope, offs, out):
         vs_g = held.tile([P, N], F32, name="vs_g")
         nc.vector.tensor_copy(out=vs_g[:], in_=vs_pool[:].indirect(offsets[:]))
 
-        pos_tp = psum.tile([P, PACK, P], F32, name="pos_tp")
+        pos_tp = psum.tile([P, PACK, P], F32, name="pos_tp", tag="pos_tp")
         pos_v = pos_g[:].rearrange("p (s t) -> p t s", t=PACK)
         for t in range(PACK):
             nc.tensor.transpose(pos_tp[:, t, :], pos_v[:, t, :], ident[:])
@@ -106,17 +107,26 @@ def tile_attend_alibi_srt_kernel(tc, qT, kT, vT, vs, pos, slope, offs, out):
         pos_row = psum.tile([P, PACK, SUB], F32, name="pos_row")
         for t in range(PACK):
             nc.tensor.transpose(pos_row[:, t, :], pos_col[:, t : t + 1].to_broadcast([P, P]), ident[:])
-        neg_bias = held.tile([P, PACK, SUB], F32, name="neg_bias")
+        neg_bias = held.tile([P, PACK, SUB], F32, name="neg_bias", tag="bias_then_values", align_bytes=64)
         nc.vector.tensor_scalar(neg_bias[:], pos_row[:], slope_col[:, 0:1], -1.0, ALU.mult, ALU.mult)
 
-        q_bf = held.tile([P, PASSES, NQ, PACK], BF16, name="q_bf", align_bytes=64)
-        for g in range(PASSES):
-            nc.scalar.copy(q_bf[:, g, :, :], q_raw[:, g, :, :].rearrange("p j q -> p q j"))
-        q_codes = held.tile([P, PASSES * NQ], U32, name="q_codes", align_bytes=64)
-        q_scales = held.tile([P, PASSES * NQ], U8, name="q_scales", align_bytes=64)
-        nc.vector.quantize_mx(
-            out=q_codes[:].bitcast(FP8X4), scales=q_scales[:], in_=q_bf[:].rearrange("p g q j -> p (g q j)")
-        )
+        q_bf = [held.tile([P, NQ, PACK], BF16, name=f"q_bf{g}", align_bytes=64) for g in range(PASSES)]
+        q_codes = [held.tile([P, NQ], U32, name=f"q_codes{g}", align_bytes=64) for g in range(PASSES)]
+        q_scales = [held.tile([P, NQ], U8, name=f"q_scales{g}", align_bytes=64) for g in range(PASSES)]
+
+        def quantise_queries(g):
+            nc.scalar.copy(q_bf[g][:], q_raw[g][:].rearrange("p j q -> p q j"))
+            nc.vector.quantize_mx(
+                out=q_codes[g][:].bitcast(FP8X4), scales=q_scales[g][:], in_=q_bf[g][:].rearrange("p q j -> p (q j)")
+            )
+
+        quantise_queries(0)
+
+        warm = psum.tile([P, PACK, P], F32, name="warm", tag="pos_tp")
+
+        def keep_warm(tile, blocks):
+            for i in range(blocks):
+                nc.tensor.transpose(warm[:, i % PACK, :], tile[:, i * P : (i + 1) * P], ident[:])
 
         for j in range(1, PACK):
             nc.vector.tensor_copy(out=g4[:, j, :], in_=k_pool[j][:].indirect(offsets[:]))
@@ -131,11 +141,14 @@ def tile_attend_alibi_srt_kernel(tc, qT, kT, vT, vs, pos, slope, offs, out):
         for j in range(2):
             nc.vector.tensor_copy(out=g2[:, j, :], in_=k_pool[PACK + j][:].indirect(offsets[:]))
         nc.scalar.copy(k_bf[1][:, :, 0:2], g2[:].rearrange("p j s -> p s j"))
+        keep_warm(k_pool[PACK + 2], 12)
         nc.vector.tensor_copy(out=k_bf[1][:, :, 2], in_=k_pool[PACK + 2][:].indirect(offsets[:]))
+        keep_warm(k_pool[PACK + 3], 12)
         for h in range(2):
             cols = slice(h * HALF, (h + 1) * HALF)
             list_part = offsets[:, h * (HALF // 16) : (h + 1) * (HALF // 16)]
             nc.vector.tensor_copy(out=k_bf[1][:, cols, 3], in_=k_pool[PACK + 3][:].indirect(list_part))
+        quantise_queries(1)
         for h in range(2):
             cols = slice(h * HALF, (h + 1) * HALF)
             nc.vector.quantize_mx(
@@ -154,6 +167,8 @@ def tile_attend_alibi_srt_kernel(tc, qT, kT, vT, vs, pos, slope, offs, out):
                 score[h][:].rearrange("q (s t) -> q t s", t=PACK),
                 ALU.subtract,
             )
+        for i in range(8):
+            nc.tensor.transpose(warm[:, i % PACK, :], neg_s[:, i % PACK, :], ident[:])
         neg_m = held.tile([NQ, 1], F32, name="neg_m")
         nc.vector.tensor_reduce(neg_m[:], neg_s[:].rearrange("q t s -> q (t s)"), AXIS.X, ALU.min)
         p = held.tile([NQ, PACK, SUB], F32, name="p")
@@ -171,7 +186,7 @@ def tile_attend_alibi_srt_kernel(tc, qT, kT, vT, vs, pos, slope, offs, out):
             for t in (2 * h, 2 * h + 1):
                 nc.tensor.transpose(w_tp[:, t, :], p[:, t, :], ident[:])
 
-        v_bf = held.tile([DV, PACK, SUB], BF16, name="v_bf")
+        v_bf = held.tile([DV, PACK, SUB], BF16, name="v_bf", tag="bias_then_values", align_bytes=64)
         nc.vector.tensor_copy(out=v_bf[:].rearrange("e t s -> e s t"), in_=v_pool[:].indirect(offsets[:]))
         v_tp = psum.tile([P, PACK, DV], BF16, name="v_tp")
         for t in range(PACK):
@@ -186,15 +201,15 @@ def tile_attend_alibi_srt_kernel(tc, qT, kT, vT, vs, pos, slope, offs, out):
             vs_col[:].unsqueeze(1).to_broadcast([P, NQ, PACK]),
             ALU.mult,
         )
-        v_codes = held.tile([P, DV], U32, name="v_codes", align_bytes=64)
-        v_scales = held.tile([P, DV], U8, name="v_scales", align_bytes=64)
-        nc.vector.quantize_mx(
-            out=v_codes[:].bitcast(FP8X4), scales=v_scales[:], in_=v_rows[:].rearrange("s e t -> s (e t)")
-        )
         w_codes = held.tile([P, NQ], U32, name="w_codes", align_bytes=64)
         w_scales = held.tile([P, NQ], U8, name="w_scales", align_bytes=64)
         nc.vector.quantize_mx(
             out=w_codes[:].bitcast(FP8X4), scales=w_scales[:], in_=w_bf[:].rearrange("s q t -> s (q t)")
+        )
+        v_codes = held.tile([P, DV], U32, name="v_codes", align_bytes=64)
+        v_scales = held.tile([P, DV], U8, name="v_scales", align_bytes=64)
+        nc.vector.quantize_mx(
+            out=v_codes[:].bitcast(FP8X4), scales=v_scales[:], in_=v_rows[:].rearrange("s e t -> s (e t)")
         )
         total = held.tile([NQ, 1], F32, name="total")
         nc.vector.tensor_tensor(total[:], l_part[:, 0:1], l_part[:, 1:2], ALU.add)

@@ -55,8 +55,9 @@ def tile_attend_alibi_srt_kernel(tc, qT, kT, vT, vs, pos, slope, offs, out):
                 k_pool.append(plane)
                 if g == 0 and j == 0:
                     nc.sync.dma_start(pos_pool[0:1, :], pos[0:1, :])
-                    nc.sync.dma_start(vs_pool[0:1, :], vs[0:1, :])
                     nc.sync.dma_start(q_raw[0][:], q_rows[0])
+                if g == 0 and j == 1:
+                    nc.sync.dma_start(vs_pool[0:1, :], vs[0:1, :])
         nc.sync.dma_start(q_raw[1][:], q_rows[1])
         v_pool = held.tile([P, T], F32, name="v_pool")
         nc.sync.dma_start(v_pool[:], vT)
@@ -83,20 +84,33 @@ def tile_attend_alibi_srt_kernel(tc, qT, kT, vT, vs, pos, slope, offs, out):
                 stop=(g == PASSES - 1),
             )
 
+        def gather_plane(out_plane, index, list_part):
+            nc.vector.tensor_copy(out=out_plane, in_=k_pool[index][:].indirect(list_part))
+
         g4 = held.tile([P, PACK, N], F32, name="g4")
-        nc.vector.tensor_copy(out=g4[:, 0, :], in_=k_pool[0][:].indirect(offsets[:]))
+        g2 = held.tile([P, 2, N], F32, name="g2")
+        gather_plane(g4[:, 0, :], 0, offsets[:])
 
         pos_g = held.tile([P, N], F32, name="pos_g")
         nc.vector.tensor_copy(out=pos_g[:], in_=pos_pool[:].indirect(offsets[:]))
-        vs_g = held.tile([P, N], F32, name="vs_g")
-        nc.vector.tensor_copy(out=vs_g[:], in_=vs_pool[:].indirect(offsets[:]))
-
         pos_tp = psum.tile([P, PACK, P], F32, name="pos_tp", tag="pos_tp")
         pos_v = pos_g[:].rearrange("p (s t) -> p t s", t=PACK)
         for t in range(PACK):
             nc.tensor.transpose(pos_tp[:, t, :], pos_v[:, t, :], ident[:])
         pos_col = held.tile([P, PACK], F32, name="pos_col")
         nc.scalar.copy(pos_col[:], pos_tp[:, :, 0])
+        pos_row = psum.tile([P, PACK, SUB], F32, name="pos_row")
+        for t in range(PACK):
+            nc.tensor.transpose(pos_row[:, t, :], pos_col[:, t : t + 1].to_broadcast([P, P]), ident[:])
+        neg_slope = held.tile([P, 1], F32, name="neg_slope")
+        nc.scalar.mul(neg_slope[:], slope_col[:], -1.0)
+        neg_bias = held.tile([P, PACK, SUB], F32, name="neg_bias", tag="bias_then_values", align_bytes=64)
+        nc.scalar.activation(out=neg_bias[:], in_=pos_row[:], func=ACT.Copy, scale=neg_slope[:, 0:1])
+
+        gather_plane(g4[:, 1, :], 1, offsets[:])
+
+        vs_g = held.tile([P, N], F32, name="vs_g")
+        nc.vector.tensor_copy(out=vs_g[:], in_=vs_pool[:].indirect(offsets[:]))
         vs_tp = psum.tile([P, PACK, P], F32, name="vs_tp")
         vs_v = vs_g[:].rearrange("p (s t) -> p t s", t=PACK)
         for t in range(PACK):
@@ -104,11 +118,7 @@ def tile_attend_alibi_srt_kernel(tc, qT, kT, vT, vs, pos, slope, offs, out):
         vs_col = held.tile([P, PACK], F32, name="vs_col")
         nc.scalar.copy(vs_col[:], vs_tp[:, :, 0])
 
-        pos_row = psum.tile([P, PACK, SUB], F32, name="pos_row")
-        for t in range(PACK):
-            nc.tensor.transpose(pos_row[:, t, :], pos_col[:, t : t + 1].to_broadcast([P, P]), ident[:])
-        neg_bias = held.tile([P, PACK, SUB], F32, name="neg_bias", tag="bias_then_values", align_bytes=64)
-        nc.vector.tensor_scalar(neg_bias[:], pos_row[:], slope_col[:, 0:1], -1.0, ALU.mult, ALU.mult)
+        gather_plane(g4[:, 2, :], 2, offsets[:])
 
         q_bf = [held.tile([P, NQ, PACK], BF16, name=f"q_bf{g}", align_bytes=64) for g in range(PASSES)]
         q_codes = [held.tile([P, NQ], U32, name=f"q_codes{g}", align_bytes=64) for g in range(PASSES)]
@@ -128,19 +138,17 @@ def tile_attend_alibi_srt_kernel(tc, qT, kT, vT, vs, pos, slope, offs, out):
             for i in range(blocks):
                 nc.tensor.transpose(warm[:, i % PACK, :], tile[:, i * P : (i + 1) * P], ident[:])
 
-        for j in range(1, PACK):
-            nc.vector.tensor_copy(out=g4[:, j, :], in_=k_pool[j][:].indirect(offsets[:]))
+        gather_plane(g4[:, 3, :], 3, offsets[:])
         nc.scalar.copy(k_bf[0][:], g4[:].rearrange("p j s -> p s j"))
+        for j in range(2):
+            gather_plane(g2[:, j, :], PACK + j, offsets[:])
+        nc.scalar.copy(k_bf[1][:, :, 0:2], g2[:].rearrange("p j s -> p s j"))
         nc.vector.quantize_mx(
             out=k_codes[0][:].bitcast(FP8X4), scales=k_scales[0][:], in_=k_bf[0][:].rearrange("p s j -> p (s j)")
         )
         for h in range(2):
             score_pass(0, h)
 
-        g2 = held.tile([P, 2, N], F32, name="g2")
-        for j in range(2):
-            nc.vector.tensor_copy(out=g2[:, j, :], in_=k_pool[PACK + j][:].indirect(offsets[:]))
-        nc.scalar.copy(k_bf[1][:, :, 0:2], g2[:].rearrange("p j s -> p s j"))
         keep_warm(k_pool[PACK + 2], 12)
         nc.vector.tensor_copy(out=k_bf[1][:, :, 2], in_=k_pool[PACK + 2][:].indirect(offsets[:]))
         keep_warm(k_pool[PACK + 3], 12)

@@ -93,7 +93,7 @@ def tile_attend_alibi_srt_kernel(tc, qT, kT, vT, vs, pos, slope, offs, out):
 
         pos_g = held.tile([P, N], F32, name="pos_g")
         nc.vector.tensor_copy(out=pos_g[:], in_=pos_pool[:].indirect(offsets[:]))
-        pos_tp = psum.tile([P, PACK, P], F32, name="pos_tp", tag="pos_tp")
+        pos_tp = psum.tile([P, PACK, P], F32, name="pos_tp")
         pos_v = pos_g[:].rearrange("p (s t) -> p t s", t=PACK)
         for t in range(PACK):
             nc.tensor.transpose(pos_tp[:, t, :], pos_v[:, t, :], ident[:])
@@ -132,12 +132,6 @@ def tile_attend_alibi_srt_kernel(tc, qT, kT, vT, vs, pos, slope, offs, out):
 
         quantise_queries(0)
 
-        warm = psum.tile([P, PACK, P], F32, name="warm", tag="pos_tp")
-
-        def keep_warm(tile, blocks):
-            for i in range(blocks):
-                nc.tensor.transpose(warm[:, i % PACK, :], tile[:, i * P : (i + 1) * P], ident[:])
-
         gather_plane(g4[:, 3, :], 3, offsets[:])
         nc.scalar.copy(k_bf[0][:], g4[:].rearrange("p j s -> p s j"))
         for j in range(2):
@@ -149,9 +143,7 @@ def tile_attend_alibi_srt_kernel(tc, qT, kT, vT, vs, pos, slope, offs, out):
         for h in range(2):
             score_pass(0, h)
 
-        keep_warm(k_pool[PACK + 2], 12)
         nc.vector.tensor_copy(out=k_bf[1][:, :, 2], in_=k_pool[PACK + 2][:].indirect(offsets[:]))
-        keep_warm(k_pool[PACK + 3], 12)
         for h in range(2):
             cols = slice(h * HALF, (h + 1) * HALF)
             list_part = offsets[:, h * (HALF // 16) : (h + 1) * (HALF // 16)]
@@ -175,8 +167,6 @@ def tile_attend_alibi_srt_kernel(tc, qT, kT, vT, vs, pos, slope, offs, out):
                 score[h][:].rearrange("q (s t) -> q t s", t=PACK),
                 ALU.subtract,
             )
-        for i in range(8):
-            nc.tensor.transpose(warm[:, i % PACK, :], neg_s[:, i % PACK, :], ident[:])
         neg_m = held.tile([NQ, 1], F32, name="neg_m")
         nc.vector.tensor_reduce(neg_m[:], neg_s[:].rearrange("q t s -> q (t s)"), AXIS.X, ALU.min)
         p = held.tile([NQ, PACK, SUB], F32, name="p")
@@ -199,6 +189,11 @@ def tile_attend_alibi_srt_kernel(tc, qT, kT, vT, vs, pos, slope, offs, out):
         v_tp = psum.tile([P, PACK, DV], BF16, name="v_tp")
         for t in range(PACK):
             nc.tensor.transpose(v_tp[:, t, :], v_bf[:, t, :], ident_bf[:])
+        total = held.tile([NQ, 1], F32, name="total")
+        nc.vector.tensor_tensor(total[:], l_part[:, 0:1], l_part[:, 1:2], ALU.add)
+        inverse = held.tile([NQ, 1], F32, name="inverse")
+        nc.vector.reciprocal(inverse[:], total[:])
+
         v_rows = held.tile([P, DV, PACK], BF16, name="v_rows", align_bytes=64)
         nc.scalar.copy(v_rows[:], v_tp[:].rearrange("s t e -> s e t"))
 
@@ -219,11 +214,6 @@ def tile_attend_alibi_srt_kernel(tc, qT, kT, vT, vs, pos, slope, offs, out):
         nc.vector.quantize_mx(
             out=v_codes[:].bitcast(FP8X4), scales=v_scales[:], in_=v_rows[:].rearrange("s e t -> s (e t)")
         )
-        total = held.tile([NQ, 1], F32, name="total")
-        nc.vector.tensor_tensor(total[:], l_part[:, 0:1], l_part[:, 1:2], ALU.add)
-        inverse = held.tile([NQ, 1], F32, name="inverse")
-        nc.vector.reciprocal(inverse[:], total[:])
-
         y = psum.tile([NQ, DV], F32, name="y")
         nc.tensor.matmul_mx(
             out=y[:],

from contextlib import ExitStack

import concourse.mybir as mybir
from concourse.masks import make_identity

P = 128
PACK = 4
D, T, N, NQ, DV = 1024, 2048, 512, 128, 128
PASSES = D // (P * PACK)
HALF = N // 2
SUB = N // PACK

F32 = mybir.dt.float32
BF16 = mybir.dt.bfloat16
U32 = mybir.dt.uint32
U16 = mybir.dt.uint16
U8 = mybir.dt.uint8
FP8X4 = mybir.dt.float8_e4m3fn_x4
ALU = mybir.AluOpType
ACT = mybir.ActivationFunctionType
AXIS = mybir.AxisListType

FLOPS = 2 * NQ * N * (D + DV)
BYTES = 4 * (D * NQ + D * T + DV * T + 2 * T + NQ + NQ * DV) + 2 * P * (N // 16)


def tile_attend_alibi_srt_kernel(tc, qT, kT, vT, vs, pos, slope, offs, out):
    nc = tc.nc
    with ExitStack() as ctx:
        held = ctx.enter_context(tc.tile_pool(name="held", bufs=1))
        psum = ctx.enter_context(tc.psum_pool(name="psum", bufs=1))

        offsets = held.tile([P, N // 16], U16, name="offsets")
        nc.sync.dma_start(offsets[:], offs)

        dummy = held.tile([P, 1], F32, name="dummy")
        nc.vector.memset(dummy[:], 0.0)
        nc.scalar.activation(out=dummy[:], in_=dummy[:], func=ACT.Exp)

        pos_pool = held.tile([P, T], F32, name="pos_pool")
        vs_pool = held.tile([P, T], F32, name="vs_pool")
        slope_col = held.tile([P, 1], F32, name="slope_col")
        nc.scalar.dma_start(slope_col[:], slope[0])
        nc.vector.memset(pos_pool[:], 0.0)
        nc.gpsimd.memset(vs_pool[:], 0.0)

        planes = kT.rearrange("(g p j) t -> g j p t", g=PASSES, j=PACK)
        k_pool = []
        q_rows = qT[0].rearrange("(g p j) q -> g p j q", g=PASSES, j=PACK)
        q_raw = [held.tile([P, PACK, NQ], F32, name=f"q_raw{g}") for g in range(PASSES)]
        for g in range(PASSES):
            for j in range(PACK):
                plane = held.tile([P, T], F32, name=f"plane{g}{j}")
                nc.sync.dma_start(plane[:], planes[g, j])
                k_pool.append(plane)
                if g == 0 and j == 0:
                    nc.sync.dma_start(pos_pool[0:1, :], pos[0:1, :])
                    nc.sync.dma_start(q_raw[0][:], q_rows[0])
                if g == 0 and j == 1:
                    nc.sync.dma_start(vs_pool[0:1, :], vs[0:1, :])
        nc.sync.dma_start(q_raw[1][:], q_rows[1])
        v_pool = held.tile([P, T], F32, name="v_pool")
        nc.sync.dma_start(v_pool[:], vT)

        ident = held.tile([P, P], F32, name="ident")
        make_identity(nc, ident[:])
        ident_bf = held.tile([P, P], BF16, name="ident_bf")
        make_identity(nc, ident_bf[:])

        score = [psum.tile([NQ, HALF], F32, name=f"score{h}") for h in range(2)]
        k_bf = [held.tile([P, N, PACK], BF16, name=f"k_bf{g}", align_bytes=64) for g in range(PASSES)]
        k_codes = [held.tile([P, N], U32, name=f"k_codes{g}", align_bytes=64) for g in range(PASSES)]
        k_scales = [held.tile([P, N], U8, name=f"k_scales{g}", align_bytes=64) for g in range(PASSES)]

        def score_pass(g, h):
            cols = slice(h * HALF, (h + 1) * HALF)
            nc.tensor.matmul_mx(
                out=score[h][:],
                lhsT=q_codes[g][:].bitcast(FP8X4),
                lhsT_scale=q_scales[g][:],
                rhs=k_codes[g][:, cols].bitcast(FP8X4),
                rhs_scale=k_scales[g][:, cols],
                start=(g == 0),
                stop=(g == PASSES - 1),
            )

        def gather_plane(out_plane, index, list_part):
            nc.vector.tensor_copy(out=out_plane, in_=k_pool[index][:].indirect(list_part))

        g4 = held.tile([P, PACK, N], F32, name="g4")
        g2 = held.tile([P, 2, N], F32, name="g2")
        gather_plane(g4[:, 0, :], 0, offsets[:])

        pos_g = held.tile([P, N], F32, name="pos_g")
        nc.vector.tensor_copy(out=pos_g[:], in_=pos_pool[:].indirect(offsets[:]))
        pos_tp = psum.tile([P, PACK, P], F32, name="pos_tp")
        pos_v = pos_g[:].rearrange("p (s t) -> p t s", t=PACK)
        for t in range(PACK):
            nc.tensor.transpose(pos_tp[:, t, :], pos_v[:, t, :], ident[:])
        pos_col = held.tile([P, PACK], F32, name="pos_col")
        nc.scalar.copy(pos_col[:], pos_tp[:, :, 0])
        pos_row = psum.tile([P, PACK, SUB], F32, name="pos_row")
        for t in range(PACK):
            nc.tensor.transpose(pos_row[:, t, :], pos_col[:, t : t + 1].to_broadcast([P, P]), ident[:])
        neg_slope = held.tile([P, 1], F32, name="neg_slope")
        nc.scalar.mul(neg_slope[:], slope_col[:], -1.0)
        neg_bias = held.tile([P, PACK, SUB], F32, name="neg_bias", tag="bias_then_values", align_bytes=64)
        nc.scalar.activation(out=neg_bias[:], in_=pos_row[:], func=ACT.Copy, scale=neg_slope[:, 0:1])

        gather_plane(g4[:, 1, :], 1, offsets[:])

        vs_g = held.tile([P, N], F32, name="vs_g")
        nc.vector.tensor_copy(out=vs_g[:], in_=vs_pool[:].indirect(offsets[:]))
        vs_tp = psum.tile([P, PACK, P], F32, name="vs_tp")
        vs_v = vs_g[:].rearrange("p (s t) -> p t s", t=PACK)
        for t in range(PACK):
            nc.tensor.transpose(vs_tp[:, t, :], vs_v[:, t, :], ident[:])
        vs_col = held.tile([P, PACK], F32, name="vs_col")
        nc.scalar.copy(vs_col[:], vs_tp[:, :, 0])

        gather_plane(g4[:, 2, :], 2, offsets[:])

        q_bf = [held.tile([P, NQ, PACK], BF16, name=f"q_bf{g}", align_bytes=64) for g in range(PASSES)]
        q_codes = [held.tile([P, NQ], U32, name=f"q_codes{g}", align_bytes=64) for g in range(PASSES)]
        q_scales = [held.tile([P, NQ], U8, name=f"q_scales{g}", align_bytes=64) for g in range(PASSES)]

        def quantise_queries(g):
            nc.scalar.copy(q_bf[g][:], q_raw[g][:].rearrange("p j q -> p q j"))
            nc.vector.quantize_mx(
                out=q_codes[g][:].bitcast(FP8X4), scales=q_scales[g][:], in_=q_bf[g][:].rearrange("p q j -> p (q j)")
            )

        quantise_queries(0)

        gather_plane(g4[:, 3, :], 3, offsets[:])
        nc.scalar.copy(k_bf[0][:], g4[:].rearrange("p j s -> p s j"))
        for j in range(2):
            gather_plane(g2[:, j, :], PACK + j, offsets[:])
        nc.scalar.copy(k_bf[1][:, :, 0:2], g2[:].rearrange("p j s -> p s j"))
        nc.vector.quantize_mx(
            out=k_codes[0][:].bitcast(FP8X4), scales=k_scales[0][:], in_=k_bf[0][:].rearrange("p s j -> p (s j)")
        )
        for h in range(2):
            score_pass(0, h)

        nc.vector.tensor_copy(out=k_bf[1][:, :, 2], in_=k_pool[PACK + 2][:].indirect(offsets[:]))
        for h in range(2):
            cols = slice(h * HALF, (h + 1) * HALF)
            list_part = offsets[:, h * (HALF // 16) : (h + 1) * (HALF // 16)]
            nc.vector.tensor_copy(out=k_bf[1][:, cols, 3], in_=k_pool[PACK + 3][:].indirect(list_part))
        quantise_queries(1)
        for h in range(2):
            cols = slice(h * HALF, (h + 1) * HALF)
            nc.vector.quantize_mx(
                out=k_codes[1][:, cols].bitcast(FP8X4),
                scales=k_scales[1][:, cols],
                in_=k_bf[1][:, cols, :].rearrange("p s j -> p (s j)"),
            )
            score_pass(1, h)

        neg_s = held.tile([NQ, PACK, SUB], F32, name="neg_s")
        for h in range(2):
            part = slice(h * (SUB // 2), (h + 1) * (SUB // 2))
            nc.vector.tensor_tensor(
                neg_s[:, :, part],
                neg_bias[:, :, part],
                score[h][:].rearrange("q (s t) -> q t s", t=PACK),
                ALU.subtract,
            )
        neg_m = held.tile([NQ, 1], F32, name="neg_m")
        nc.vector.tensor_reduce(neg_m[:], neg_s[:].rearrange("q t s -> q (t s)"), AXIS.X, ALU.min)
        p = held.tile([NQ, PACK, SUB], F32, name="p")
        l_part = held.tile([NQ, 2], F32, name="l_part")
        w_tp = psum.tile([P, PACK, NQ], F32, name="w_tp")
        for h in range(2):
            nc.scalar.activation(
                out=p[:, 2 * h : 2 * h + 2, :],
                in_=neg_s[:, 2 * h : 2 * h + 2, :],
                func=ACT.Exp,
                bias=neg_m[:, 0:1],
                scale=-1.0,
                accum_out=l_part[:, h : h + 1],
            )
            for t in (2 * h, 2 * h + 1):
                nc.tensor.transpose(w_tp[:, t, :], p[:, t, :], ident[:])

        v_bf = held.tile([DV, PACK, SUB], BF16, name="v_bf", tag="bias_then_values", align_bytes=64)
        nc.vector.tensor_copy(out=v_bf[:].rearrange("e t s -> e s t"), in_=v_pool[:].indirect(offsets[:]))
        v_tp = psum.tile([P, PACK, DV], BF16, name="v_tp")
        for t in range(PACK):
            nc.tensor.transpose(v_tp[:, t, :], v_bf[:, t, :], ident_bf[:])
        total = held.tile([NQ, 1], F32, name="total")
        nc.vector.tensor_tensor(total[:], l_part[:, 0:1], l_part[:, 1:2], ALU.add)
        inverse = held.tile([NQ, 1], F32, name="inverse")
        nc.vector.reciprocal(inverse[:], total[:])

        v_rows = held.tile([P, DV, PACK], BF16, name="v_rows", align_bytes=64)
        nc.scalar.copy(v_rows[:], v_tp[:].rearrange("s t e -> s e t"))

        w_bf = held.tile([P, NQ, PACK], BF16, name="w_bf", align_bytes=64)
        nc.vector.tensor_tensor(
            w_bf[:],
            w_tp[:].rearrange("s t q -> s q t"),
            vs_col[:].unsqueeze(1).to_broadcast([P, NQ, PACK]),
            ALU.mult,
        )
        w_codes = held.tile([P, NQ], U32, name="w_codes", align_bytes=64)
        w_scales = held.tile([P, NQ], U8, name="w_scales", align_bytes=64)
        nc.vector.quantize_mx(
            out=w_codes[:].bitcast(FP8X4), scales=w_scales[:], in_=w_bf[:].rearrange("s q t -> s (q t)")
        )
        v_codes = held.tile([P, DV], U32, name="v_codes", align_bytes=64)
        v_scales = held.tile([P, DV], U8, name="v_scales", align_bytes=64)
        nc.vector.quantize_mx(
            out=v_codes[:].bitcast(FP8X4), scales=v_scales[:], in_=v_rows[:].rearrange("s e t -> s (e t)")
        )
        y = psum.tile([NQ, DV], F32, name="y")
        nc.tensor.matmul_mx(
            out=y[:],
            lhsT=w_codes[:].bitcast(FP8X4),
            lhsT_scale=w_scales[:],
            rhs=v_codes[:].bitcast(FP8X4),
            rhs_scale=v_scales[:],
            start=True,
            stop=True,
        )
        result = held.tile([NQ, DV], F32, name="result")
        nc.vector.tensor_scalar(result[:], y[:], inverse[:, 0:1], None, ALU.mult)
        nc.sync.dma_start(out[0], result[:])
